import numpy as np, ml_dtypes
CORES = [13,21,141,149]
N = 4
import mx_ref
NC, G = 128, 4
BF = ml_dtypes.bfloat16
def cut(t, i, w=512):
    return t[:, w * i:w * i + w]
def tile(rs):
    return np.stack(rs, axis=2).reshape(128, -1).astype(BF)
def layer(w, X):
    out = []
    for i in range(G):
        for t in range(len(X)):
            p = mx_ref.matmul(mx_ref.quantize(cut(w, len(X) * i + t)), X[t])
            z = p if t == 0 else z + p
        out.append(z)
    return out
def scaled(Z, s):
    return [z * s for z in Z]
def setup_inputs(rng):
    def f(*shape):
        return mx_ref.flush((rng.standard_normal(shape, dtype=np.float32) * np.exp2(rng.integers(-2, 3, shape[:-1] + (1,)))).astype(BF))
    return {"x": f(N, 128, 4 * NC), "w1": f(N, 128, G * 512), "w2": f(N, 128, 2 * 512)}
def setup_inputs_blocks(rng):
    d = setup_inputs(rng)
    for k in ("w2",): d[k] = mx_ref.spread(d[k], rng, 4)
    for k in ("x", "w1"): d[k] = mx_ref.spread(d[k], rng, 2)
    return d
def setup_inputs_wide(rng):
    d = setup_inputs(rng)
    for k in ("x", "w1", "w2"): d[k] = mx_ref.flush((d[k].astype(np.float32) * np.exp2(rng.integers(-3, 4, (N, 1, 1))).astype(np.float32)).astype(BF))
    return d
def reference(x, w1, w2, own=None):
    Z = [layer(w1[r], [mx_ref.quantize(x[r])]) for r in range(N)]
    a = max(float(np.abs(z).max()) for r in range(N) for z in Z[r])
    s = np.float32(1 / a)
    h = np.stack([tile(scaled(Z[r], s)) for r in range(N)])
    use = h if own is None else own["h"]
    H = [mx_ref.quantize(use[j]) for j in range(N)]
    y = np.zeros((N, 128, NC), np.float32)
    for r in range(N):
        y[r] = mx_ref.matmul(mx_ref.quantize(cut(w2[r], 0)), H[r]) + mx_ref.matmul(mx_ref.quantize(cut(w2[r], 1)), H[(r + 1) % N])
    return {"h": h, "y": y}

@@ -1,0 +1,220 @@
+from concourse.bass import DstId, RemoteDMATransfer
+from concourse.mybir import dt, AluOpType, AxisListType, ActivationFunctionType
+
+WORLD = 256
+C = 128
+E = 512
+B = 512
+
+SCRATCH = {
+    "xs": ("sbuf", [128, E], "bfloat16"),
+    "w1s": ("sbuf", [128, 4 * E], "bfloat16"),
+    "w2s": ("sbuf", [128, 2 * E], "bfloat16"),
+    "xq": ("sbuf", [128, C], "float8_e4m3fn_x4"),
+    "xp": ("sbuf", [128, C], "uint8"),
+    "w1q": ("sbuf", [128, 4 * C], "float8_e4m3fn_x4"),
+    "w1p": ("sbuf", [128, 4 * C], "uint8"),
+    "w2q": ("sbuf", [128, 2 * C], "float8_e4m3fn_x4"),
+    "w2p": ("sbuf", [128, 2 * C], "uint8"),
+    "ht": ("sbuf", [128, E], "bfloat16"),
+    "hq": ("sbuf", [128, C], "float8_e4m3fn_x4"),
+    "hp": ("sbuf", [128, C], "uint8"),
+    "inq": ("sbuf", [128, C], "float8_e4m3fn_x4"),
+    "inp": ("sbuf", [128, C], "uint8"),
+    "ones": ("sbuf", [128, 128], "float32"),
+    "eye": ("sbuf", [128, 128], "float32"),
+    "part": ("sbuf", [128, 4], "float32"),
+    "part3": ("sbuf", [128, 1], "float32"),
+    "own": ("sbuf", [128, 1], "float32"),
+    "rel": ("sbuf", [128, 1], "float32"),
+    "arr": ("sbuf", [128, 4], "float32"),
+    "wide": ("sbuf", [128, 128], "float32"),
+    "amax": ("sbuf", [128, 1], "float32"),
+    "inv": ("sbuf", [128, 1], "float32"),
+    "ys": ("sbuf", [128, C], "float32"),
+    "zp": ("psum", [128, 4 * B], "float32"),
+    "tp": ("psum", [128, B], "float32"),
+    "yp": ("psum", [128, B], "float32"),
+}
+SEMAPHORES = ["ld_x", "ld_wa", "ld_wb", "ld_w2", "st_h", "st_y", "vec", "ten", "act", "poo",
+              "m_rel", "m_peer", "m_far", "q_rel", "p_rel", "h_in", "l_max", "l_h", "l_rel"]
+
+
+def bits(mask):
+    return [e for e in range(16) if mask >> e & 1]
+
+
+def pack(engines):
+    return sum(1 << e for e in engines)
+
+
+def plan(cores, rank, topo):
+    me = cores[rank]
+    n = len(cores)
+    order = [(rank + k) % n for k in range(1, n)]
+    peers = [k for k in order if topo.may_write(me, cores[k])]
+    far = [k for k in order if not topo.may_write(me, cores[k])]
+    able = [c for c in range(WORLD)
+            if topo.host(c) == topo.host(me) and topo.chip(c) == topo.chip(me) and c not in cores
+            and all(topo.may_write(c, cores[k]) for k in far)]
+    near_relay = [c for c in able if topo.die(c) == topo.die(me)][0]
+    far_relay = [c for c in able if topo.die(c) != topo.die(me)][0]
+    return peers, far, [near_relay, far_relay]
+
+
+def engines(me, peer, relays, topo):
+    off = bits(topo.mask(me, peer))
+    on = bits(topo.mask(me, relays[0]))
+    rest = [e for e in on if e not in off]
+    return off[0::2], [rest[0::2], rest[1::2]], [on[0::2], on[1::2]], on
+
+
+def rank_program(g, core, T, topo):
+    cores = list(T.cores)
+    n = len(cores)
+    rank = T.rank_of(core)
+    if rank is None:
+        for r in range(n):
+            peers, far, relays = plan(cores, r, topo)
+            if core in relays:
+                relay_program(g, core, T, topo, cores, r, peers, far, relays)
+        return
+    peers, far, relays = plan(cores, rank, topo)
+    S = T.sem
+    V, P, A, Y = g.vector, g.tensor, g.scalar, g.sync
+    e_peer, e_rel, e_half, e_all = engines(core, cores[peers[0]], relays, topo)
+    X = AxisListType.X
+
+    def z(i, w=C):
+        return T.zp[:, B * i:B * i + w]
+
+    A.dma_start(T.w1s[:, 0:3 * E], T.w1[:, 0:3 * E]).then_inc(S.ld_wa, 16)
+    Y.dma_start(T.xs[:], T.x[:]).then_inc(S.ld_x, 16)
+    Y.dma_start(T.w1s[:, 3 * E:4 * E], T.w1[:, 3 * E:4 * E]).then_inc(S.ld_wb, 16)
+    Y.wait_ge(S.l_max, len(e_peer) + len(e_rel[0]) + len(e_rel[1]))
+    Y.dma_start(T.w2s[:], T.w2[:]).then_inc(S.ld_w2, 16)
+    Y.wait_ge(S.vec, 17)
+    Y.wait_ge(S.act, 2)
+    Y.wait_ge(S.l_h, len(e_half[0]) + len(e_half[1]) + len(e_all))
+    Y.dma_start(T.h[:], T.ht[:]).then_inc(S.st_h, 16)
+    Y.wait_ge(S.vec, 20)
+    Y.dma_start(T.y[:], T.ys[:]).then_inc(S.st_y, 16)
+    Y.wait_ge(S.st_h, 16)
+    Y.wait_ge(S.st_y, 16)
+
+    V.memset(T.ones[:], 1.0).then_inc(S.vec, 1)
+    V.wait_ge(S.ld_x, 16)
+    V.quantize_mx(T.xq[:, 0:C], T.xp[:, 0:C], T.xs[:, 0:E]).then_inc(S.vec, 1)
+
+    def q1(i):
+        V.quantize_mx(T.w1q[:, C * i:C * i + C], T.w1p[:, C * i:C * i + C], T.w1s[:, E * i:E * i + E]).then_inc(S.vec, 1)
+
+    V.wait_ge(S.ld_wa, 16)
+    for i in range(3):
+        q1(i)
+    for i in range(3):
+        V.wait_ge(S.ten, i + 1)
+        V.tensor_reduce(T.part[:, i:i + 1], z(i), X, AluOpType.max, apply_absolute_value=True).then_inc(S.vec, 1)
+    V.wait_ge(S.vec, 8)
+    V.tensor_reduce(T.part3[:], T.part[:, 0:3], X, AluOpType.max).then_inc(S.vec, 1)
+    V.wait_ge(S.ld_wb, 16)
+    q1(3)
+    V.wait_ge(S.ten, 5)
+    V.tensor_reduce(T.own[:], z(3, C + 1), X, AluOpType.max, apply_absolute_value=True).then_inc(S.vec, 1)
+    V.wait_ge(S.vec, 11)
+    V.wait_ge(S.m_peer, len(e_peer))
+    V.tensor_scalar(T.wide[:], T.ones[:], T.own[:], T.arr[:, 0:1], AluOpType.mult, AluOpType.max).then_inc(S.vec, 1)
+    V.wait_ge(S.vec, 12)
+    V.wait_ge(S.m_far, sum(len(bits(topo.mask(plan(cores, k, topo)[2][0], core))) for k in far))
+    V.tensor_scalar(T.wide[:], T.wide[:], T.arr[:, 1:2], T.arr[:, 2:3], AluOpType.max, AluOpType.max).then_inc(S.vec, 1)
+    V.wait_ge(S.ten, 6)
+    V.tensor_reduce(T.amax[:], T.tp[:, 0:128], X, AluOpType.max).then_inc(S.vec, 1)
+    V.wait_ge(S.vec, 14)
+    V.reciprocal(T.inv[:], T.amax[:]).then_inc(S.vec, 1)
+    V.wait_ge(S.vec, 15)
+    for b in (0, 1):
+        V.tensor_scalar(T.ht[:, b:E:4], z(b), T.inv[:], None, AluOpType.mult).then_inc(S.vec, 1)
+    V.wait_ge(S.vec, 17)
+    V.wait_ge(S.act, 2)
+    V.quantize_mx(T.hq[:, 0:C], T.hp[:, 0:C], T.ht[:, 0:E]).then_inc(S.vec, 1)
+    V.wait_ge(S.ld_w2, 16)
+    V.quantize_mx(T.w2q[:, 0:2 * C], T.w2p[:, 0:2 * C], T.w2s[:, 0:2 * E]).then_inc(S.vec, 1)
+    V.wait_ge(S.ten, 8)
+    V.tensor_copy(T.ys[:], T.yp[:, 0:C]).then_inc(S.vec, 1)
+
+    A.wait_ge(S.vec, 15)
+    for b in (2, 3):
+        A.activation(T.ht[:, b:E:4], z(b), ActivationFunctionType.Copy, scale=T.inv[:]).then_inc(S.act, 1)
+
+    def m1(i):
+        P.matmul_mx(z(i), T.w1q[:, C * i:C * i + C], T.w1p[:, C * i:C * i + C], T.xq[:, 0:C], T.xp[:, 0:C],
+                    True, True).then_inc(S.ten, 1)
+
+    for i in range(3):
+        P.wait_ge(S.vec, 3 + i)
+        m1(i)
+    P.wait_ge(S.poo, 1)
+    P.wait_ge(S.vec, 9)
+    P.matmul(T.zp[:, 3 * B + C:3 * B + C + 1], T.eye[:], T.part3[:], True, True).then_inc(S.ten, 1)
+    P.wait_ge(S.vec, 10)
+    m1(3)
+    P.wait_ge(S.vec, 13)
+    P.transpose(T.tp[:, 0:128], T.wide[:], T.eye[:]).then_inc(S.ten, 1)
+    P.wait_ge(S.vec, 19)
+    P.matmul_mx(T.yp[:, 0:C], T.w2q[:, 0:C], T.w2p[:, 0:C], T.hq[:, 0:C], T.hp[:, 0:C], True, False).then_inc(S.ten, 1)
+    src = (rank + 1) % n
+    sr = plan(cores, src, topo)[2]
+    P.wait_ge(S.h_in, sum(len(bits(topo.mask(c, core))) for c in (sr[0], sr[1], sr[0])))
+    P.matmul_mx(T.yp[:, 0:C], T.w2q[:, C:2 * C], T.w2p[:, C:2 * C], T.inq[:, 0:C], T.inp[:, 0:C], False, True).then_inc(S.ten, 1)
+
+    g.wait_ge(S.vec, 1)
+    g.affine_select(T.eye[:], T.ones[:], [[-1, 128]], AluOpType.is_equal, 0.0, 0, 1).then_inc(S.poo, 1)
+    to = []
+    for c, e in zip(relays, e_rel):
+        rid, pid = topo.addr(c, core)
+        to.append(RemoteDMATransfer(dst_ids=[DstId(rid=rid, pnc=pid)], dma_engine_mask=pack(e), remote_sem=S.m_rel,
+                                    src=T.own[:], dst=T.rel[:]))
+    rid, pid = topo.addr(cores[peers[0]], core)
+    to.append(RemoteDMATransfer(dst_ids=[DstId(rid=rid, pnc=pid)], dma_engine_mask=pack(e_peer), remote_sem=S.m_peer,
+                                src=T.own[:], dst=T.arr[:, 0:1]))
+    g.wait_ge(S.vec, 11)
+    g.remote_dma_fused(to, local_sem=S.l_max)
+    half = []
+    for k, (c, e) in enumerate(zip(relays, e_half)):
+        rid, pid = topo.addr(c, core)
+        a, b = k * C // 2, (k + 1) * C // 2
+        half.append(RemoteDMATransfer(dst_ids=[DstId(rid=rid, pnc=pid)], dma_engine_mask=pack(e), remote_sem=S.q_rel,
+                                      src=T.hq[:, a:b].bitcast(dt.uint8), dst=T.inq[:, a:b].bitcast(dt.uint8)))
+    rid, pid = topo.addr(relays[0], core)
+    g.wait_ge(S.vec, 18)
+    g.remote_dma_fused(half, local_sem=S.l_h)
+    g.remote_dma(T.inp[:, 0:C], T.hp[:, 0:C], S.p_rel, S.l_h, pid, rid, pack(e_all))
+    g.wait_ge(S.vec, 20)
+    g.wait_ge(S.ten, 8)
+
+
+def relay_program(g, core, T, topo, cores, r, peers, far, relays):
+    S = T.sem
+    n = len(cores)
+    k = relays.index(core)
+    _, e_rel, e_half, e_all = engines(cores[r], cores[peers[0]], relays, topo)
+    sent = 0
+    to = cores[far[k]]
+    slot = 1 + plan(cores, far[k], topo)[1].index(r)
+    rid, pid = topo.addr(to, core)
+    mask = topo.mask(core, to)
+    g.wait_ge(S.m_rel, len(e_rel[k]))
+    g.remote_dma(T.arr[:, slot:slot + 1], T.rel[:], S.m_far, S.l_rel, pid, rid, mask)
+    sent += len(bits(mask))
+    to = cores[(r - 1) % n]
+    rid, pid = topo.addr(to, core)
+    mask = topo.mask(core, to)
+    a, b = k * C // 2, (k + 1) * C // 2
+    g.wait_ge(S.q_rel, len(e_half[k]))
+    g.remote_dma(T.inq[:, a:b].bitcast(dt.uint8), T.inq[:, a:b].bitcast(dt.uint8), S.h_in, S.l_rel, pid, rid, mask)
+    sent += len(bits(mask))
+    if k == 0:
+        g.wait_ge(S.p_rel, len(e_all))
+        g.remote_dma(T.inp[:, 0:C], T.inp[:, 0:C], S.h_in, S.l_rel, pid, rid, mask)
+        sent += len(bits(mask))
+    g.wait_ge(S.l_rel, sent)

@@ -23,10 +23,12 @@ SCRATCH = {
     "inp": ("sbuf", [128, C], "uint8"),
     "ones": ("sbuf", [128, 128], "float32"),
     "eye": ("sbuf", [128, 128], "float32"),
-    "part": ("sbuf", [128, 4], "float32"),
-    "part3": ("sbuf", [128, 1], "float32"),
+    "first": ("sbuf", [128, 1], "float32"),
+    "part": ("sbuf", [128, 3], "float32"),
+    "last": ("sbuf", [128, 1], "float32"),
     "own": ("sbuf", [128, 1], "float32"),
-    "rel": ("sbuf", [128, 1], "float32"),
+    "rel0": ("sbuf", [128, 1], "float32"),
+    "rel1": ("sbuf", [128, 1], "float32"),
     "arr": ("sbuf", [128, 4], "float32"),
     "wide": ("sbuf", [128, 128], "float32"),
     "amax": ("sbuf", [128, 1], "float32"),
@@ -36,16 +38,12 @@ SCRATCH = {
     "tp": ("psum", [128, B], "float32"),
     "yp": ("psum", [128, B], "float32"),
 }
-SEMAPHORES = ["ld_x", "ld_wa", "ld_wb", "ld_w2", "st_h", "st_y", "vec", "ten", "act", "poo",
-              "m_rel", "m_peer", "m_far", "q_rel", "p_rel", "h_in", "l_max", "l_h", "l_rel"]
+SEMAPHORES = ["ld_x", "ld_0", "ld_2", "ld_w2", "st_h", "st_y", "vec", "ten", "act", "poo",
+              "m_rel0", "m_rel1", "m_peer", "m_far", "q_rel", "p_rel", "h_in", "l_max", "l_h", "l_rel"]
 
 
 def bits(mask):
     return [e for e in range(16) if mask >> e & 1]
-
-
-def pack(engines):
-    return sum(1 << e for e in engines)
 
 
 def plan(cores, rank, topo):
@@ -54,19 +52,15 @@ def plan(cores, rank, topo):
     order = [(rank + k) % n for k in range(1, n)]
     peers = [k for k in order if topo.may_write(me, cores[k])]
     far = [k for k in order if not topo.may_write(me, cores[k])]
-    able = [c for c in range(WORLD)
-            if topo.host(c) == topo.host(me) and topo.chip(c) == topo.chip(me) and c not in cores
-            and all(topo.may_write(c, cores[k]) for k in far)]
-    near_relay = [c for c in able if topo.die(c) == topo.die(me)][0]
-    far_relay = [c for c in able if topo.die(c) != topo.die(me)][0]
-    return peers, far, [near_relay, far_relay]
+    relay = [c for c in range(WORLD)
+             if topo.host(c) == topo.host(me) and topo.chip(c) == topo.chip(me) and topo.die(c) == topo.die(me)
+             and c not in cores and all(topo.may_write(c, cores[k]) for k in far)][0]
+    return peers, far, relay
 
 
-def engines(me, peer, relays, topo):
-    off = bits(topo.mask(me, peer))
-    on = bits(topo.mask(me, relays[0]))
-    rest = [e for e in on if e not in off]
-    return off[0::2], [rest[0::2], rest[1::2]], [on[0::2], on[1::2]], on
+def lanes(me, peer, relay, topo):
+    on, off = topo.mask(me, relay), topo.mask(me, peer)
+    return on, off, on & ~off
 
 
 def rank_program(g, core, T, topo):
@@ -75,29 +69,30 @@ def rank_program(g, core, T, topo):
     rank = T.rank_of(core)
     if rank is None:
         for r in range(n):
-            peers, far, relays = plan(cores, r, topo)
-            if core in relays:
-                relay_program(g, core, T, topo, cores, r, peers, far, relays)
+            peers, far, relay = plan(cores, r, topo)
+            if core == relay:
+                relay_program(g, core, T, topo, cores, r, peers, far)
         return
-    peers, far, relays = plan(cores, rank, topo)
+    peers, far, relay = plan(cores, rank, topo)
     S = T.sem
     V, P, A, Y = g.vector, g.tensor, g.scalar, g.sync
-    e_peer, e_rel, e_half, e_all = engines(core, cores[peers[0]], relays, topo)
+    on, off, rest = lanes(core, cores[peers[0]], relay, topo)
+    n_on, n_off, n_rest = len(bits(on)), len(bits(off)), len(bits(rest))
     X = AxisListType.X
 
-    def z(i, w=C):
-        return T.zp[:, B * i:B * i + w]
+    def z(i):
+        return T.zp[:, B * i:B * i + C]
 
-    A.dma_start(T.w1s[:, 0:3 * E], T.w1[:, 0:3 * E]).then_inc(S.ld_wa, 16)
     Y.dma_start(T.xs[:], T.x[:]).then_inc(S.ld_x, 16)
-    Y.dma_start(T.w1s[:, 3 * E:4 * E], T.w1[:, 3 * E:4 * E]).then_inc(S.ld_wb, 16)
-    Y.wait_ge(S.l_max, len(e_peer) + len(e_rel[0]) + len(e_rel[1]))
+    A.dma_start(T.w1s[:, 0:2 * E], T.w1[:, 0:2 * E]).then_inc(S.ld_0, 16)
+    Y.dma_start(T.w1s[:, 2 * E:4 * E], T.w1[:, 2 * E:4 * E]).then_inc(S.ld_2, 16)
+    Y.wait_ge(S.l_max, 2 * n_rest + n_off)
     Y.dma_start(T.w2s[:], T.w2[:]).then_inc(S.ld_w2, 16)
-    Y.wait_ge(S.vec, 17)
+    Y.wait_ge(S.vec, 18)
     Y.wait_ge(S.act, 2)
-    Y.wait_ge(S.l_h, len(e_half[0]) + len(e_half[1]) + len(e_all))
+    Y.wait_ge(S.l_h, 2 * n_on)
     Y.dma_start(T.h[:], T.ht[:]).then_inc(S.st_h, 16)
-    Y.wait_ge(S.vec, 20)
+    Y.wait_ge(S.vec, 21)
     Y.dma_start(T.y[:], T.ys[:]).then_inc(S.st_y, 16)
     Y.wait_ge(S.st_h, 16)
     Y.wait_ge(S.st_y, 16)
@@ -109,112 +104,101 @@ def rank_program(g, core, T, topo):
     def q1(i):
         V.quantize_mx(T.w1q[:, C * i:C * i + C], T.w1p[:, C * i:C * i + C], T.w1s[:, E * i:E * i + E]).then_inc(S.vec, 1)
 
-    V.wait_ge(S.ld_wa, 16)
-    for i in range(3):
-        q1(i)
-    for i in range(3):
+    def red(i):
         V.wait_ge(S.ten, i + 1)
-        V.tensor_reduce(T.part[:, i:i + 1], z(i), X, AluOpType.max, apply_absolute_value=True).then_inc(S.vec, 1)
-    V.wait_ge(S.vec, 8)
-    V.tensor_reduce(T.part3[:], T.part[:, 0:3], X, AluOpType.max).then_inc(S.vec, 1)
-    V.wait_ge(S.ld_wb, 16)
+        out = T.part[:, i - 1:i] if i else T.first[:]
+        V.tensor_reduce(out, z(i), X, AluOpType.max, apply_absolute_value=True).then_inc(S.vec, 1)
+
+    V.wait_ge(S.ld_0, 16)
+    q1(0)
+    q1(1)
+    red(0)
+    red(1)
+    V.wait_ge(S.ld_2, 16)
+    q1(2)
     q1(3)
-    V.wait_ge(S.ten, 5)
-    V.tensor_reduce(T.own[:], z(3, C + 1), X, AluOpType.max, apply_absolute_value=True).then_inc(S.vec, 1)
+    red(2)
+    red(3)
+    V.wait_ge(S.vec, 10)
+    V.tensor_reduce(T.last[:], T.part[:], X, AluOpType.max).then_inc(S.vec, 1)
     V.wait_ge(S.vec, 11)
-    V.wait_ge(S.m_peer, len(e_peer))
-    V.tensor_scalar(T.wide[:], T.ones[:], T.own[:], T.arr[:, 0:1], AluOpType.mult, AluOpType.max).then_inc(S.vec, 1)
+    V.tensor_tensor(T.own[:], T.first[:], T.last[:], AluOpType.max).then_inc(S.vec, 1)
     V.wait_ge(S.vec, 12)
-    V.wait_ge(S.m_far, sum(len(bits(topo.mask(plan(cores, k, topo)[2][0], core))) for k in far))
+    V.wait_ge(S.m_peer, n_off)
+    V.tensor_scalar(T.wide[:], T.ones[:], T.own[:], T.arr[:, 0:1], AluOpType.mult, AluOpType.max).then_inc(S.vec, 1)
+    V.wait_ge(S.vec, 13)
+    V.wait_ge(S.m_far, sum(len(bits(topo.mask(plan(cores, k, topo)[2], core))) for k in far))
     V.tensor_scalar(T.wide[:], T.wide[:], T.arr[:, 1:2], T.arr[:, 2:3], AluOpType.max, AluOpType.max).then_inc(S.vec, 1)
-    V.wait_ge(S.ten, 6)
+    V.wait_ge(S.ten, 5)
     V.tensor_reduce(T.amax[:], T.tp[:, 0:128], X, AluOpType.max).then_inc(S.vec, 1)
-    V.wait_ge(S.vec, 14)
-    V.reciprocal(T.inv[:], T.amax[:]).then_inc(S.vec, 1)
     V.wait_ge(S.vec, 15)
+    V.reciprocal(T.inv[:], T.amax[:]).then_inc(S.vec, 1)
+    V.wait_ge(S.vec, 16)
     for b in (0, 1):
         V.tensor_scalar(T.ht[:, b:E:4], z(b), T.inv[:], None, AluOpType.mult).then_inc(S.vec, 1)
-    V.wait_ge(S.vec, 17)
+    V.wait_ge(S.vec, 18)
     V.wait_ge(S.act, 2)
     V.quantize_mx(T.hq[:, 0:C], T.hp[:, 0:C], T.ht[:, 0:E]).then_inc(S.vec, 1)
     V.wait_ge(S.ld_w2, 16)
     V.quantize_mx(T.w2q[:, 0:2 * C], T.w2p[:, 0:2 * C], T.w2s[:, 0:2 * E]).then_inc(S.vec, 1)
-    V.wait_ge(S.ten, 8)
+    V.wait_ge(S.ten, 7)
     V.tensor_copy(T.ys[:], T.yp[:, 0:C]).then_inc(S.vec, 1)
 
-    A.wait_ge(S.vec, 15)
+    A.wait_ge(S.vec, 16)
     for b in (2, 3):
         A.activation(T.ht[:, b:E:4], z(b), ActivationFunctionType.Copy, scale=T.inv[:]).then_inc(S.act, 1)
 
-    def m1(i):
+    for i, v in enumerate((3, 4, 7, 8)):
+        P.wait_ge(S.vec, v)
         P.matmul_mx(z(i), T.w1q[:, C * i:C * i + C], T.w1p[:, C * i:C * i + C], T.xq[:, 0:C], T.xp[:, 0:C],
                     True, True).then_inc(S.ten, 1)
-
-    for i in range(3):
-        P.wait_ge(S.vec, 3 + i)
-        m1(i)
     P.wait_ge(S.poo, 1)
-    P.wait_ge(S.vec, 9)
-    P.matmul(T.zp[:, 3 * B + C:3 * B + C + 1], T.eye[:], T.part3[:], True, True).then_inc(S.ten, 1)
-    P.wait_ge(S.vec, 10)
-    m1(3)
-    P.wait_ge(S.vec, 13)
+    P.wait_ge(S.vec, 14)
     P.transpose(T.tp[:, 0:128], T.wide[:], T.eye[:]).then_inc(S.ten, 1)
-    P.wait_ge(S.vec, 19)
+    P.wait_ge(S.vec, 20)
     P.matmul_mx(T.yp[:, 0:C], T.w2q[:, 0:C], T.w2p[:, 0:C], T.hq[:, 0:C], T.hp[:, 0:C], True, False).then_inc(S.ten, 1)
-    src = (rank + 1) % n
-    sr = plan(cores, src, topo)[2]
-    P.wait_ge(S.h_in, sum(len(bits(topo.mask(c, core))) for c in (sr[0], sr[1], sr[0])))
+    P.wait_ge(S.h_in, 2 * len(bits(topo.mask(plan(cores, (rank + 1) % n, topo)[2], core))))
     P.matmul_mx(T.yp[:, 0:C], T.w2q[:, C:2 * C], T.w2p[:, C:2 * C], T.inq[:, 0:C], T.inp[:, 0:C], False, True).then_inc(S.ten, 1)
 
     g.wait_ge(S.vec, 1)
     g.affine_select(T.eye[:], T.ones[:], [[-1, 128]], AluOpType.is_equal, 0.0, 0, 1).then_inc(S.poo, 1)
-    to = []
-    for c, e in zip(relays, e_rel):
-        rid, pid = topo.addr(c, core)
-        to.append(RemoteDMATransfer(dst_ids=[DstId(rid=rid, pnc=pid)], dma_engine_mask=pack(e), remote_sem=S.m_rel,
-                                    src=T.own[:], dst=T.rel[:]))
-    rid, pid = topo.addr(cores[peers[0]], core)
-    to.append(RemoteDMATransfer(dst_ids=[DstId(rid=rid, pnc=pid)], dma_engine_mask=pack(e_peer), remote_sem=S.m_peer,
-                                src=T.own[:], dst=T.arr[:, 0:1]))
+    rid, pid = topo.addr(relay, core)
+    prid, ppid = topo.addr(cores[peers[0]], core)
+    g.wait_ge(S.vec, 5)
+    g.remote_dma(T.rel0[:], T.first[:], S.m_rel0, S.l_max, pid, rid, rest)
     g.wait_ge(S.vec, 11)
-    g.remote_dma_fused(to, local_sem=S.l_max)
-    half = []
-    for k, (c, e) in enumerate(zip(relays, e_half)):
-        rid, pid = topo.addr(c, core)
-        a, b = k * C // 2, (k + 1) * C // 2
-        half.append(RemoteDMATransfer(dst_ids=[DstId(rid=rid, pnc=pid)], dma_engine_mask=pack(e), remote_sem=S.q_rel,
-                                      src=T.hq[:, a:b].bitcast(dt.uint8), dst=T.inq[:, a:b].bitcast(dt.uint8)))
-    rid, pid = topo.addr(relays[0], core)
-    g.wait_ge(S.vec, 18)
-    g.remote_dma_fused(half, local_sem=S.l_h)
-    g.remote_dma(T.inp[:, 0:C], T.hp[:, 0:C], S.p_rel, S.l_h, pid, rid, pack(e_all))
-    g.wait_ge(S.vec, 20)
-    g.wait_ge(S.ten, 8)
+    g.remote_dma(T.rel1[:], T.last[:], S.m_rel1, S.l_max, pid, rid, rest)
+    g.wait_ge(S.vec, 12)
+    g.remote_dma(T.arr[:, 0:1], T.own[:], S.m_peer, S.l_max, ppid, prid, off)
+    g.wait_ge(S.vec, 19)
+    g.remote_dma(T.inq[:, 0:C].bitcast(dt.uint8), T.hq[:, 0:C].bitcast(dt.uint8), S.q_rel, S.l_h, pid, rid, on)
+    g.remote_dma(T.inp[:, 0:C], T.hp[:, 0:C], S.p_rel, S.l_h, pid, rid, on)
+    g.wait_ge(S.vec, 21)
+    g.wait_ge(S.ten, 7)
 
 
-def relay_program(g, core, T, topo, cores, r, peers, far, relays):
+def relay_program(g, core, T, topo, cores, r, peers, far):
     S = T.sem
     n = len(cores)
-    k = relays.index(core)
-    _, e_rel, e_half, e_all = engines(cores[r], cores[peers[0]], relays, topo)
-    sent = 0
-    to = cores[far[k]]
-    slot = 1 + plan(cores, far[k], topo)[1].index(r)
-    rid, pid = topo.addr(to, core)
-    mask = topo.mask(core, to)
-    g.wait_ge(S.m_rel, len(e_rel[k]))
-    g.remote_dma(T.arr[:, slot:slot + 1], T.rel[:], S.m_far, S.l_rel, pid, rid, mask)
-    sent += len(bits(mask))
+    on, off, rest = lanes(cores[r], cores[peers[0]], core, topo)
+    to = [cores[k] for k in far]
+    ids = []
+    for d in to:
+        rid, pid = topo.addr(d, core)
+        ids.append(DstId(rid=rid, pnc=pid))
+    slots = [1 + plan(cores, k, topo)[1].index(r) for k in far]
+    mask = topo.mask(core, to[0])
+    g.vector.wait_ge(S.m_rel0, len(bits(rest)))
+    g.vector.wait_ge(S.m_rel1, len(bits(rest)))
+    g.vector.tensor_tensor(T.own[:], T.rel0[:], T.rel1[:], AluOpType.max).then_inc(S.vec, 1)
+    g.wait_ge(S.vec, 1)
+    g.remote_dma_fused([RemoteDMATransfer(dst_ids=ids, dma_engine_mask=mask, remote_sem=S.m_far,
+                                          src=T.own[:], dsts=[T.arr[:, s:s + 1] for s in slots])],
+                       local_sem=S.l_rel)
     to = cores[(r - 1) % n]
     rid, pid = topo.addr(to, core)
-    mask = topo.mask(core, to)
-    a, b = k * C // 2, (k + 1) * C // 2
-    g.wait_ge(S.q_rel, len(e_half[k]))
-    g.remote_dma(T.inq[:, a:b].bitcast(dt.uint8), T.inq[:, a:b].bitcast(dt.uint8), S.h_in, S.l_rel, pid, rid, mask)
-    sent += len(bits(mask))
-    if k == 0:
-        g.wait_ge(S.p_rel, len(e_all))
-        g.remote_dma(T.inp[:, 0:C], T.inp[:, 0:C], S.h_in, S.l_rel, pid, rid, mask)
-        sent += len(bits(mask))
-    g.wait_ge(S.l_rel, sent)
+    g.wait_ge(S.q_rel, len(bits(on)))
+    g.remote_dma(T.inq[:, 0:C].bitcast(dt.uint8), T.inq[:, 0:C].bitcast(dt.uint8), S.h_in, S.l_rel, pid, rid, mask)
+    g.wait_ge(S.p_rel, len(bits(on)))
+    g.remote_dma(T.inp[:, 0:C], T.inp[:, 0:C], S.h_in, S.l_rel, pid, rid, mask)
+    g.wait_ge(S.l_rel, 3 * len(bits(mask)))

from concourse.bass import DstId, RemoteDMATransfer
from concourse.mybir import dt, AluOpType, AxisListType, ActivationFunctionType

WORLD = 256
C = 128
E = 512
B = 512

SCRATCH = {
    "xs": ("sbuf", [128, E], "bfloat16"),
    "w1s": ("sbuf", [128, 4 * E], "bfloat16"),
    "w2s": ("sbuf", [128, 2 * E], "bfloat16"),
    "xq": ("sbuf", [128, C], "float8_e4m3fn_x4"),
    "xp": ("sbuf", [128, C], "uint8"),
    "w1q": ("sbuf", [128, 4 * C], "float8_e4m3fn_x4"),
    "w1p": ("sbuf", [128, 4 * C], "uint8"),
    "w2q": ("sbuf", [128, 2 * C], "float8_e4m3fn_x4"),
    "w2p": ("sbuf", [128, 2 * C], "uint8"),
    "ht": ("sbuf", [128, E], "bfloat16"),
    "hq": ("sbuf", [128, C], "float8_e4m3fn_x4"),
    "hp": ("sbuf", [128, C], "uint8"),
    "inq": ("sbuf", [128, C], "float8_e4m3fn_x4"),
    "inp": ("sbuf", [128, C], "uint8"),
    "ones": ("sbuf", [128, 128], "float32"),
    "eye": ("sbuf", [128, 128], "float32"),
    "first": ("sbuf", [128, 1], "float32"),
    "part": ("sbuf", [128, 3], "float32"),
    "last": ("sbuf", [128, 1], "float32"),
    "own": ("sbuf", [128, 1], "float32"),
    "rel0": ("sbuf", [128, 1], "float32"),
    "rel1": ("sbuf", [128, 1], "float32"),
    "arr": ("sbuf", [128, 4], "float32"),
    "wide": ("sbuf", [128, 128], "float32"),
    "amax": ("sbuf", [128, 1], "float32"),
    "inv": ("sbuf", [128, 1], "float32"),
    "ys": ("sbuf", [128, C], "float32"),
    "zp": ("psum", [128, 4 * B], "float32"),
    "tp": ("psum", [128, B], "float32"),
    "yp": ("psum", [128, B], "float32"),
}
SEMAPHORES = ["ld_x", "ld_0", "ld_2", "ld_w2", "st_h", "st_y", "vec", "ten", "act", "poo",
              "m_rel0", "m_rel1", "m_peer", "m_far", "q_rel", "p_rel", "h_in", "l_max", "l_h", "l_rel"]


def bits(mask):
    return [e for e in range(16) if mask >> e & 1]


def plan(cores, rank, topo):
    me = cores[rank]
    n = len(cores)
    order = [(rank + k) % n for k in range(1, n)]
    peers = [k for k in order if topo.may_write(me, cores[k])]
    far = [k for k in order if not topo.may_write(me, cores[k])]
    relay = [c for c in range(WORLD)
             if topo.host(c) == topo.host(me) and topo.chip(c) == topo.chip(me) and topo.die(c) == topo.die(me)
             and c not in cores and all(topo.may_write(c, cores[k]) for k in far)][0]
    return peers, far, relay


def lanes(me, peer, relay, topo):
    on, off = topo.mask(me, relay), topo.mask(me, peer)
    return on, off, on & ~off


def rank_program(g, core, T, topo):
    cores = list(T.cores)
    n = len(cores)
    rank = T.rank_of(core)
    if rank is None:
        for r in range(n):
            peers, far, relay = plan(cores, r, topo)
            if core == relay:
                relay_program(g, core, T, topo, cores, r, peers, far)
        return
    peers, far, relay = plan(cores, rank, topo)
    S = T.sem
    V, P, A, Y = g.vector, g.tensor, g.scalar, g.sync
    on, off, rest = lanes(core, cores[peers[0]], relay, topo)
    n_on, n_off, n_rest = len(bits(on)), len(bits(off)), len(bits(rest))
    X = AxisListType.X

    def z(i):
        return T.zp[:, B * i:B * i + C]

    Y.dma_start(T.xs[:], T.x[:]).then_inc(S.ld_x, 16)
    A.dma_start(T.w1s[:, 0:2 * E], T.w1[:, 0:2 * E]).then_inc(S.ld_0, 16)
    Y.dma_start(T.w1s[:, 2 * E:4 * E], T.w1[:, 2 * E:4 * E]).then_inc(S.ld_2, 16)
    Y.wait_ge(S.l_max, 2 * n_rest + n_off)
    Y.dma_start(T.w2s[:], T.w2[:]).then_inc(S.ld_w2, 16)
    Y.wait_ge(S.vec, 18)
    Y.wait_ge(S.act, 2)
    Y.wait_ge(S.l_h, 2 * n_on)
    Y.dma_start(T.h[:], T.ht[:]).then_inc(S.st_h, 16)
    Y.wait_ge(S.vec, 21)
    Y.dma_start(T.y[:], T.ys[:]).then_inc(S.st_y, 16)
    Y.wait_ge(S.st_h, 16)
    Y.wait_ge(S.st_y, 16)

    V.memset(T.ones[:], 1.0).then_inc(S.vec, 1)
    V.wait_ge(S.ld_x, 16)
    V.quantize_mx(T.xq[:, 0:C], T.xp[:, 0:C], T.xs[:, 0:E]).then_inc(S.vec, 1)

    def q1(i):
        V.quantize_mx(T.w1q[:, C * i:C * i + C], T.w1p[:, C * i:C * i + C], T.w1s[:, E * i:E * i + E]).then_inc(S.vec, 1)

    def red(i):
        V.wait_ge(S.ten, i + 1)
        out = T.part[:, i - 1:i] if i else T.first[:]
        V.tensor_reduce(out, z(i), X, AluOpType.max, apply_absolute_value=True).then_inc(S.vec, 1)

    V.wait_ge(S.ld_0, 16)
    q1(0)
    q1(1)
    red(0)
    red(1)
    V.wait_ge(S.ld_2, 16)
    q1(2)
    q1(3)
    red(2)
    red(3)
    V.wait_ge(S.vec, 10)
    V.tensor_reduce(T.last[:], T.part[:], X, AluOpType.max).then_inc(S.vec, 1)
    V.wait_ge(S.vec, 11)
    V.tensor_tensor(T.own[:], T.first[:], T.last[:], AluOpType.max).then_inc(S.vec, 1)
    V.wait_ge(S.vec, 12)
    V.wait_ge(S.m_peer, n_off)
    V.tensor_scalar(T.wide[:], T.ones[:], T.own[:], T.arr[:, 0:1], AluOpType.mult, AluOpType.max).then_inc(S.vec, 1)
    V.wait_ge(S.vec, 13)
    V.wait_ge(S.m_far, sum(len(bits(topo.mask(plan(cores, k, topo)[2], core))) for k in far))
    V.tensor_scalar(T.wide[:], T.wide[:], T.arr[:, 1:2], T.arr[:, 2:3], AluOpType.max, AluOpType.max).then_inc(S.vec, 1)
    V.wait_ge(S.ten, 5)
    V.tensor_reduce(T.amax[:], T.tp[:, 0:128], X, AluOpType.max).then_inc(S.vec, 1)
    V.wait_ge(S.vec, 15)
    V.reciprocal(T.inv[:], T.amax[:]).then_inc(S.vec, 1)
    V.wait_ge(S.vec, 16)
    for b in (0, 1):
        V.tensor_scalar(T.ht[:, b:E:4], z(b), T.inv[:], None, AluOpType.mult).then_inc(S.vec, 1)
    V.wait_ge(S.vec, 18)
    V.wait_ge(S.act, 2)
    V.quantize_mx(T.hq[:, 0:C], T.hp[:, 0:C], T.ht[:, 0:E]).then_inc(S.vec, 1)
    V.wait_ge(S.ld_w2, 16)
    V.quantize_mx(T.w2q[:, 0:2 * C], T.w2p[:, 0:2 * C], T.w2s[:, 0:2 * E]).then_inc(S.vec, 1)
    V.wait_ge(S.ten, 7)
    V.tensor_copy(T.ys[:], T.yp[:, 0:C]).then_inc(S.vec, 1)

    A.wait_ge(S.vec, 16)
    for b in (2, 3):
        A.activation(T.ht[:, b:E:4], z(b), ActivationFunctionType.Copy, scale=T.inv[:]).then_inc(S.act, 1)

    for i, v in enumerate((3, 4, 7, 8)):
        P.wait_ge(S.vec, v)
        P.matmul_mx(z(i), T.w1q[:, C * i:C * i + C], T.w1p[:, C * i:C * i + C], T.xq[:, 0:C], T.xp[:, 0:C],
                    True, True).then_inc(S.ten, 1)
    P.wait_ge(S.poo, 1)
    P.wait_ge(S.vec, 14)
    P.transpose(T.tp[:, 0:128], T.wide[:], T.eye[:]).then_inc(S.ten, 1)
    P.wait_ge(S.vec, 20)
    P.matmul_mx(T.yp[:, 0:C], T.w2q[:, 0:C], T.w2p[:, 0:C], T.hq[:, 0:C], T.hp[:, 0:C], True, False).then_inc(S.ten, 1)
    P.wait_ge(S.h_in, 2 * len(bits(topo.mask(plan(cores, (rank + 1) % n, topo)[2], core))))
    P.matmul_mx(T.yp[:, 0:C], T.w2q[:, C:2 * C], T.w2p[:, C:2 * C], T.inq[:, 0:C], T.inp[:, 0:C], False, True).then_inc(S.ten, 1)

    g.wait_ge(S.vec, 1)
    g.affine_select(T.eye[:], T.ones[:], [[-1, 128]], AluOpType.is_equal, 0.0, 0, 1).then_inc(S.poo, 1)
    rid, pid = topo.addr(relay, core)
    prid, ppid = topo.addr(cores[peers[0]], core)
    g.wait_ge(S.vec, 5)
    g.remote_dma(T.rel0[:], T.first[:], S.m_rel0, S.l_max, pid, rid, rest)
    g.wait_ge(S.vec, 11)
    g.remote_dma(T.rel1[:], T.last[:], S.m_rel1, S.l_max, pid, rid, rest)
    g.wait_ge(S.vec, 12)
    g.remote_dma(T.arr[:, 0:1], T.own[:], S.m_peer, S.l_max, ppid, prid, off)
    g.wait_ge(S.vec, 19)
    g.remote_dma(T.inq[:, 0:C].bitcast(dt.uint8), T.hq[:, 0:C].bitcast(dt.uint8), S.q_rel, S.l_h, pid, rid, on)
    g.remote_dma(T.inp[:, 0:C], T.hp[:, 0:C], S.p_rel, S.l_h, pid, rid, on)
    g.wait_ge(S.vec, 21)
    g.wait_ge(S.ten, 7)


def relay_program(g, core, T, topo, cores, r, peers, far):
    S = T.sem
    n = len(cores)
    on, off, rest = lanes(cores[r], cores[peers[0]], core, topo)
    to = [cores[k] for k in far]
    ids = []
    for d in to:
        rid, pid = topo.addr(d, core)
        ids.append(DstId(rid=rid, pnc=pid))
    slots = [1 + plan(cores, k, topo)[1].index(r) for k in far]
    mask = topo.mask(core, to[0])
    g.vector.wait_ge(S.m_rel0, len(bits(rest)))
    g.vector.wait_ge(S.m_rel1, len(bits(rest)))
    g.vector.tensor_tensor(T.own[:], T.rel0[:], T.rel1[:], AluOpType.max).then_inc(S.vec, 1)
    g.wait_ge(S.vec, 1)
    g.remote_dma_fused([RemoteDMATransfer(dst_ids=ids, dma_engine_mask=mask, remote_sem=S.m_far,
                                          src=T.own[:], dsts=[T.arr[:, s:s + 1] for s in slots])],
                       local_sem=S.l_rel)
    to = cores[(r - 1) % n]
    rid, pid = topo.addr(to, core)
    g.wait_ge(S.q_rel, len(bits(on)))
    g.remote_dma(T.inq[:, 0:C].bitcast(dt.uint8), T.inq[:, 0:C].bitcast(dt.uint8), S.h_in, S.l_rel, pid, rid, mask)
    g.wait_ge(S.p_rel, len(bits(on)))
    g.remote_dma(T.inp[:, 0:C], T.inp[:, 0:C], S.h_in, S.l_rel, pid, rid, mask)
    g.wait_ge(S.l_rel, 3 * len(bits(mask)))
